import numpy as np
CORES = [129,145,193,257,273,321,385,401,449]
N = 9
TK = 256
D = 128 * N
EPS = 0.01
def setup_inputs(rng):
    return {"x": (rng.standard_normal((N, 128, TK), dtype=np.float32) * (0.5 + np.abs(rng.standard_normal((1, 1, TK), dtype=np.float32))) + rng.standard_normal((1, 1, TK), dtype=np.float32))}
def setup_inputs_big(rng):
    d = setup_inputs(rng)
    for k in ("x",): d[k] = (d[k].astype(np.float32) * 1024.0).astype(d[k].dtype)
    return d
def setup_inputs_small(rng):
    d = setup_inputs(rng)
    for k in ("x",): d[k] = (d[k].astype(np.float32) * (1 / 1024.0)).astype(d[k].dtype)
    return d
def setup_inputs_apart(rng):
    d = setup_inputs(rng)
    f = (10.0 ** rng.permutation(np.linspace(-1.5, 1.5, N))).astype(np.float32).reshape(N, 1, 1)
    for k in ("x",): d[k] = (d[k].astype(np.float32) * f).astype(d[k].dtype)
    return d
def setup_inputs_mixed(rng):
    d = setup_inputs(rng)
    f = (10.0 ** rng.uniform(-3, 3, (1, 1, TK))).astype(np.float32); shape = rng.integers(3, size=(1, 1, TK))
    for k in ("x",):
        x = d[k].astype(np.float32)
        m = x.mean(axis=(0, 1), keepdims=True); level = m + np.sign(x - m) * np.abs(x - m).mean(axis=(0, 1), keepdims=True) * rng.uniform(0.9, 1.1, x.shape).astype(np.float32)
        other = x * np.where(rng.random(x.shape) < 0.5, 0.1, 1.0).astype(np.float32)
        d[k] = (np.where(shape == 1, level, np.where(shape == 2, other, x)) * f).astype(d[k].dtype)
    return d
def setup_inputs_offset(rng):
    d = setup_inputs(rng)
    x = d["x"]; spread = x.std(axis=(0, 1), keepdims=True)
    d["x"] = (x + spread * rng.uniform(16, 48, (1, 1, TK)) * rng.choice([-1.0, 1.0], (1, 1, TK))).astype(np.float32)
    return d
def reference(x):
    X = x.astype(np.float64)
    mu = X.sum(axis=(0, 1)) / D
    Z = X - mu
    Z = Z / np.sqrt((Z ** 2).sum(axis=(0, 1)) / D + EPS)
    return {"y": Z.astype(np.float32)}

@@ -1,0 +1,164 @@
+from concourse.bass import DstId, RemoteDMATransfer
+from concourse.mybir import AluOpType, AxisListType, ActivationFunctionType
+
+NR = 9
+TK = 256
+HB = 128
+EPS = 0.01
+W = 4
+
+SCRATCH = {
+    "xs":   ("sbuf", [128, TK], "float32"),
+    "ones": ("sbuf", [128, 128], "float32"),
+    "idn":  ("sbuf", [128, 132], "float32"),
+    "stat": ("sbuf", [128, W], "float32"),
+    "land": ("sbuf", [128, W * NR], "float32"),
+    "junk": ("sbuf", [128, 2 * HB + 32], "float32"),
+    "sm":   ("sbuf", [128, 16], "float32"),
+    "yt":   ("sbuf", [128, TK], "float32"),
+    "ys":   ("sbuf", [128, TK], "float32"),
+    "pt0":  ("psum", [128, 512], "float32"),
+    "pt1":  ("psum", [128, 512], "float32"),
+    "py0":  ("psum", [128, 512], "float32"),
+    "py1":  ("psum", [128, 512], "float32"),
+}
+SEMAPHORES = ["ld", "ca", "cb", "t0", "t1", "n0", "n1", "st", "arr", "sent", "r0", "r1", "qs", "qe", "nm", "bb", "sq",
+              "rc", "y0", "y1", "u0", "u1", "c0", "c1", "so0", "so1"]
+
+
+def _plan(cores, topo):
+    hubs = [c for c in cores if all(topo.may_write(c, d) and topo.may_write(d, c) for d in cores if d != c)]
+    leaves = [c for c in cores if c not in hubs]
+    serve = {h: [] for h in hubs}
+    for host in sorted({topo.host(l) for l in leaves}):
+        free = list(hubs)
+        for l in [l for l in leaves if topo.host(l) == host]:
+            if not free:
+                free = list(hubs)
+            same = [h for h in free if topo.chip(h) == topo.chip(l)]
+            h = same[0] if same else free[0]
+            free.remove(h)
+            serve[h].append(l)
+    return hubs, leaves, serve
+
+
+def _engines(topo, src, dsts, n):
+    m = topo.mask(src, dsts[0])
+    for d in dsts[1:]:
+        m &= topo.mask(src, d)
+    out, k, b = 0, 0, 0
+    while k < n and (m >> b):
+        if (m >> b) & 1:
+            out |= 1 << b
+            k += 1
+        b += 1
+    return out, k
+
+
+def _send(g, T, topo, core, dsts, src, dst, n_eng):
+    mask, k = _engines(topo, core, dsts, n_eng)
+    ids = []
+    for d in dsts:
+        rid, pid = topo.addr(d, core)
+        ids.append(DstId(rid=rid, pnc=pid))
+    g.remote_dma_fused([RemoteDMATransfer(dst_ids=ids, dma_engine_mask=mask, remote_sem=T.sem.arr,
+                                          srcs=[src], dsts=[dst for _ in dsts], alu_op=0)], local_sem=T.sem.sent)
+    return k
+
+
+def rank_program(g, core, T, topo):
+    rank = T.rank_of(core)
+    if rank is None:
+        return
+    cores = list(T.cores)
+    hubs, leaves, serve = _plan(cores, topo)
+    is_hub = core in hubs
+    S = T.sem
+    V, A, P = g.vector, g.scalar, g.tensor
+    ADD, MUL = AluOpType.add, AluOpType.mult
+    F = ActivationFunctionType
+    NE = 8
+    pt = [T.pt0, T.pt1]
+    py = [T.py0, T.py1]
+    tsem, nsem, rsem = [S.t0, S.t1], [S.n0, S.n1], [S.r0, S.r1]
+    ysem, usem, csem, osem = [S.y0, S.y1], [S.u0, S.u1], [S.c0, S.c1], [S.so0, S.so1]
+    own, o = (T.land, W * rank) if is_hub else (T.stat, 0)
+
+    g.sync.dma_start(T.xs[:, :], T.x[:, :]).then_inc(S.ld, 16)
+    V.memset(T.ones[:, :], 1.0).then_inc(S.ca, 1)
+    V.memset(T.idn[:, 128:129], -1.0 / 128.0).then_inc(S.cb, 1)
+    g.wait_ge(S.ca, 1)
+    g.affine_select(T.idn[:, 0:128], T.ones[:, :], [[-1, 128]], AluOpType.is_equal, 0.0, 0, 1).then_inc(S.cb, 1)
+
+    P.wait_ge(S.cb, 2)
+    P.wait_ge(S.ld, 16)
+    for h in range(2):
+        P.matmul(pt[h][:, 0:129], T.xs[:, HB * h:HB * (h + 1)], T.idn[:, 0:129], True, True).then_inc(tsem[h], 1)
+    for h in range(2):
+        V.wait_ge(tsem[h], 1)
+        V.tensor_copy(own[:, o + h:o + h + 1], pt[h][:, 128:129]).then_inc(nsem[h], 1)
+    for h in range(2):
+        A.wait_ge(nsem[h], 1)
+        A.activation(T.junk[:, HB * h:HB * (h + 1)], pt[h][:, 0:128], F.Square, bias=own[:, o + h:o + h + 1], scale=1.0,
+                     accum_out=own[:, o + 2 + h:o + 3 + h]).then_inc(S.st, 1)
+
+    g.wait_ge(S.n0, 1)
+    g.wait_ge(S.n1, 1)
+    g.wait_ge(S.st, 2)
+    slot = T.land[:, W * rank:W * (rank + 1)]
+    if is_hub:
+        sent = _send(g, T, topo, core, [h for h in hubs if h != core], slot, slot, NE)
+        need = NE * (len(cores) - 1)
+        g.wait_ge(S.arr, need)
+        if serve[core]:
+            sent += _send(g, T, topo, core, serve[core], T.land[:, :], T.land[:, :], NE)
+    else:
+        sent = _send(g, T, topo, core, hubs, T.stat[:, :], slot, NE)
+        need = NE
+
+    sm, L = T.sm, T.land
+    n_all = W * NR
+    V.wait_ge(S.arr, need)
+    V.wait_ge(S.n0, 1)
+    V.wait_ge(S.n1, 1)
+    V.wait_ge(S.st, 2)
+    for h in range(2):
+        V.tensor_reduce(sm[:, h:h + 1], L[:, h:n_all:W], AxisListType.X, ADD, negate=True).then_inc(rsem[h], 1)
+    for h in range(2):
+        V.tensor_reduce(sm[:, 2 + h:3 + h], L[:, 2 + h:n_all:W], AxisListType.X, ADD).then_inc(S.qs, 1)
+    V.wait_ge(S.qs, 2)
+    V.tensor_scalar(sm[:, 4:6], sm[:, 2:4], 1.0 / (128.0 * NR), EPS, MUL, ADD).then_inc(S.qe, 1)
+    V.wait_ge(S.r0, 1)
+    V.wait_ge(S.r1, 1)
+    V.tensor_scalar(sm[:, 6:8], sm[:, 0:2], -1.0 / NR, None, MUL).then_inc(S.nm, 1)
+
+    A.wait_ge(S.arr, need)
+    A.wait_ge(S.st, 2)
+    for h in range(2):
+        A.wait_ge(rsem[h], 1)
+        A.activation(T.junk[:, 2 * HB + 16 * h:2 * HB + 16 * h + NR], L[:, h:n_all:W], F.Square, bias=sm[:, h:h + 1],
+                     scale=float(NR), accum_out=sm[:, 8 + h:9 + h]).then_inc(S.bb, 1)
+    A.wait_ge(S.bb, 2)
+    A.wait_ge(S.qe, 1)
+    for h in range(2):
+        A.activation(sm[:, 10 + h:11 + h], sm[:, 8 + h:9 + h], F.Sqrt, bias=sm[:, 4 + h:5 + h],
+                     scale=128.0 / (NR * NR * 128.0 * NR)).then_inc(S.sq, 1)
+
+    V.wait_ge(S.sq, 2)
+    V.reciprocal(sm[:, 12:14], sm[:, 10:12]).then_inc(S.rc, 1)
+    V.wait_ge(S.rc, 1)
+    V.wait_ge(S.nm, 1)
+    for h in range(2):
+        V.tensor_scalar(T.yt[:, HB * h:HB * (h + 1)], pt[h][:, 0:128], sm[:, 6 + h:7 + h], sm[:, 12 + h:13 + h],
+                        ADD, MUL).then_inc(ysem[h], 1)
+    for h in range(2):
+        P.wait_ge(ysem[h], 1)
+        P.matmul(py[h][:, 0:128], T.yt[:, HB * h:HB * (h + 1)], T.idn[:, 0:128], True, True).then_inc(usem[h], 1)
+    for h in range(2):
+        V.wait_ge(usem[h], 1)
+        V.tensor_copy(T.ys[:, HB * h:HB * (h + 1)], py[h][:, 0:128]).then_inc(csem[h], 1)
+    for h, q in ((0, g.sync), (1, g.scalar)):
+        q.wait_ge(csem[h], 1)
+        q.dma_start(T.y[:, HB * h:HB * (h + 1)], T.ys[:, HB * h:HB * (h + 1)]).then_inc(osem[h], 16)
+        q.wait_ge(osem[h], 16)
+    g.wait_ge(S.sent, sent)

@@ -14,7 +14,7 @@ SCRATCH = {
     "stat": ("sbuf", [128, W], "float32"),
     "land": ("sbuf", [128, W * NR], "float32"),
     "junk": ("sbuf", [128, 2 * HB + 32], "float32"),
-    "sm":   ("sbuf", [128, 16], "float32"),
+    "sm":   ("sbuf", [128, 32], "float32"),
     "yt":   ("sbuf", [128, TK], "float32"),
     "ys":   ("sbuf", [128, TK], "float32"),
     "pt0":  ("psum", [128, 512], "float32"),
@@ -23,7 +23,7 @@ SCRATCH = {
     "py1":  ("psum", [128, 512], "float32"),
 }
 SEMAPHORES = ["ld", "ca", "cb", "t0", "t1", "n0", "n1", "st", "arr", "sent", "r0", "r1", "qs", "qe", "nm", "bb", "sq",
-              "rc", "y0", "y1", "u0", "u1", "c0", "c1", "so0", "so1"]
+              "rc", "rs", "ia", "ib", "ic", "ie", "y0", "y1", "u0", "u1", "c0", "c1", "so0", "so1"]
 
 
 def _plan(cores, topo):
@@ -118,6 +118,18 @@ def rank_program(g, core, T, topo):
 
     sm, L = T.sm, T.land
     n_all = W * NR
+    A.wait_ge(S.st, 2)
+    A.activation(sm[:, 16:18], own[:, o + 2:o + 4], F.Sqrt, bias=EPS, scale=1.0 / (128.0 * NR)).then_inc(S.ia, 1)
+    V.wait_ge(S.ia, 1)
+    V.reciprocal(sm[:, 18:20], sm[:, 16:18]).then_inc(S.ib, 1)
+    V.wait_ge(S.ib, 1)
+    V.tensor_tensor(sm[:, 20:22], sm[:, 18:20], sm[:, 18:20], MUL).then_inc(S.ic, 1)
+    V.wait_ge(S.ic, 1)
+    V.tensor_scalar(sm[:, 22:24], sm[:, 20:22], 1.0 / float(NR * NR * NR), None, MUL).then_inc(S.ie, 1)
+    V.tensor_scalar(sm[:, 24:26], sm[:, 20:22], 1.0 / (128.0 * NR), None, MUL).then_inc(S.ie, 1)
+    V.tensor_scalar(sm[:, 26:28], sm[:, 20:22], EPS, None, MUL).then_inc(S.ie, 1)
+    V.wait_ge(S.ie, 3)
+
     V.wait_ge(S.arr, need)
     V.wait_ge(S.n0, 1)
     V.wait_ge(S.n1, 1)
@@ -127,29 +139,33 @@ def rank_program(g, core, T, topo):
     for h in range(2):
         V.tensor_reduce(sm[:, 2 + h:3 + h], L[:, 2 + h:n_all:W], AxisListType.X, ADD).then_inc(S.qs, 1)
     V.wait_ge(S.qs, 2)
-    V.tensor_scalar(sm[:, 4:6], sm[:, 2:4], 1.0 / (128.0 * NR), EPS, MUL, ADD).then_inc(S.qe, 1)
+    for h in range(2):
+        V.tensor_scalar(sm[:, 4 + h:5 + h], sm[:, 2 + h:3 + h], sm[:, 24 + h:25 + h], sm[:, 26 + h:27 + h],
+                        MUL, ADD).then_inc(S.qe, 1)
     V.wait_ge(S.r0, 1)
     V.wait_ge(S.r1, 1)
     V.tensor_scalar(sm[:, 6:8], sm[:, 0:2], -1.0 / NR, None, MUL).then_inc(S.nm, 1)
 
     A.wait_ge(S.arr, need)
-    A.wait_ge(S.st, 2)
     for h in range(2):
         A.wait_ge(rsem[h], 1)
         A.activation(T.junk[:, 2 * HB + 16 * h:2 * HB + 16 * h + NR], L[:, h:n_all:W], F.Square, bias=sm[:, h:h + 1],
                      scale=float(NR), accum_out=sm[:, 8 + h:9 + h]).then_inc(S.bb, 1)
     A.wait_ge(S.bb, 2)
-    A.wait_ge(S.qe, 1)
+    A.wait_ge(S.qe, 2)
+    A.wait_ge(S.ie, 3)
     for h in range(2):
         A.activation(sm[:, 10 + h:11 + h], sm[:, 8 + h:9 + h], F.Sqrt, bias=sm[:, 4 + h:5 + h],
-                     scale=128.0 / (NR * NR * 128.0 * NR)).then_inc(S.sq, 1)
+                     scale=sm[:, 22 + h:23 + h]).then_inc(S.sq, 1)
 
     V.wait_ge(S.sq, 2)
     V.reciprocal(sm[:, 12:14], sm[:, 10:12]).then_inc(S.rc, 1)
     V.wait_ge(S.rc, 1)
+    V.tensor_tensor(sm[:, 14:16], sm[:, 12:14], sm[:, 18:20], MUL).then_inc(S.rs, 1)
+    V.wait_ge(S.rs, 1)
     V.wait_ge(S.nm, 1)
     for h in range(2):
-        V.tensor_scalar(T.yt[:, HB * h:HB * (h + 1)], pt[h][:, 0:128], sm[:, 6 + h:7 + h], sm[:, 12 + h:13 + h],
+        V.tensor_scalar(T.yt[:, HB * h:HB * (h + 1)], pt[h][:, 0:128], sm[:, 6 + h:7 + h], sm[:, 14 + h:15 + h],
                         ADD, MUL).then_inc(ysem[h], 1)
     for h in range(2):
         P.wait_ge(ysem[h], 1)

@@ -4,6 +4,7 @@ from concourse.mybir import AluOpType, AxisListType, ActivationFunctionType
 NR = 9
 TK = 256
 HB = 128
+FG = 64
 EPS = 0.01
 W = 4
 
@@ -13,6 +14,7 @@ SCRATCH = {
     "idn":  ("sbuf", [128, 132], "float32"),
     "stat": ("sbuf", [128, W], "float32"),
     "land": ("sbuf", [128, W * NR], "float32"),
+    "res":  ("sbuf", [128, W], "float32"),
     "junk": ("sbuf", [128, 2 * HB + 32], "float32"),
     "sm":   ("sbuf", [128, 32], "float32"),
     "yt":   ("sbuf", [128, TK], "float32"),
@@ -22,23 +24,20 @@ SCRATCH = {
     "py0":  ("psum", [128, 512], "float32"),
     "py1":  ("psum", [128, 512], "float32"),
 }
-SEMAPHORES = ["ld", "ca", "cb", "t0", "t1", "n0", "n1", "st", "arr", "sent", "r0", "r1", "qs", "qe", "nm", "bb", "sq",
-              "rc", "rs", "ia", "ib", "ic", "ie", "y0", "y1", "u0", "u1", "c0", "c1", "so0", "so1"]
+SEMAPHORES = ["la", "lb", "ca", "cb", "t0", "t1", "n0", "n1", "st", "arr", "sent", "r0", "r1", "qs", "qe", "nm", "bb",
+              "sq", "rc", "rs", "ia", "ib", "ic", "ie", "y0", "y1", "u0", "u1", "c0", "c1", "so0", "so1"]
 
 
 def _plan(cores, topo):
     hubs = [c for c in cores if all(topo.may_write(c, d) and topo.may_write(d, c) for d in cores if d != c)]
     leaves = [c for c in cores if c not in hubs]
     serve = {h: [] for h in hubs}
-    for host in sorted({topo.host(l) for l in leaves}):
-        free = list(hubs)
-        for l in [l for l in leaves if topo.host(l) == host]:
-            if not free:
-                free = list(hubs)
-            same = [h for h in free if topo.chip(h) == topo.chip(l)]
-            h = same[0] if same else free[0]
-            free.remove(h)
-            serve[h].append(l)
+    near = [l for l in leaves if topo.rack(topo.host(l)) == topo.rack(topo.host(hubs[0]))]
+    for l in near + [l for l in leaves if l not in near]:
+        level = min(hubs.index(h) + len(serve[h]) for h in hubs)
+        cand = [h for h in hubs if hubs.index(h) + len(serve[h]) == level]
+        same = [h for h in cand if topo.chip(h) == topo.chip(l)]
+        serve[(same or cand)[0]].append(l)
     return hubs, leaves, serve
 
 
@@ -83,93 +82,109 @@ def rank_program(g, core, T, topo):
     tsem, nsem, rsem = [S.t0, S.t1], [S.n0, S.n1], [S.r0, S.r1]
     ysem, usem, csem, osem = [S.y0, S.y1], [S.u0, S.u1], [S.c0, S.c1], [S.so0, S.so1]
     own, o = (T.land, W * rank) if is_hub else (T.stat, 0)
+    X0, X1 = 1, 1 + 128
 
-    g.sync.dma_start(T.xs[:, :], T.x[:, :]).then_inc(S.ld, 16)
+    g.sync.dma_start(T.xs[0:FG, :], T.x[0:FG, :]).then_inc(S.la, 16)
+    g.scalar.dma_start(T.xs[FG:128, :], T.x[FG:128, :]).then_inc(S.lb, 16)
     V.memset(T.ones[:, :], 1.0).then_inc(S.ca, 1)
-    V.memset(T.idn[:, 128:129], -1.0 / 128.0).then_inc(S.cb, 1)
+    V.memset(T.idn[:, 0:1], -1.0 / 128.0).then_inc(S.cb, 1)
+    V.memset(T.idn[:, X1:X1 + 1], -1.0 / 128.0).then_inc(S.cb, 1)
     g.wait_ge(S.ca, 1)
-    g.affine_select(T.idn[:, 0:128], T.ones[:, :], [[-1, 128]], AluOpType.is_equal, 0.0, 0, 1).then_inc(S.cb, 1)
+    g.affine_select(T.idn[:, X0:X1], T.ones[:, :], [[-1, 128]], AluOpType.is_equal, 0.0, 0, 1).then_inc(S.cb, 1)
 
-    P.wait_ge(S.cb, 2)
-    P.wait_ge(S.ld, 16)
+    P.wait_ge(S.cb, 3)
+    P.wait_ge(S.la, 16)
     for h in range(2):
-        P.matmul(pt[h][:, 0:129], T.xs[:, HB * h:HB * (h + 1)], T.idn[:, 0:129], True, True).then_inc(tsem[h], 1)
+        P.matmul(pt[h][:, 0:X0 + FG], T.xs[0:FG, HB * h:HB * (h + 1)], T.idn[0:FG, 0:X0 + FG],
+                 True, True).then_inc(tsem[h], 1)
+    P.wait_ge(S.lb, 16)
     for h in range(2):
-        V.wait_ge(tsem[h], 1)
-        V.tensor_copy(own[:, o + h:o + h + 1], pt[h][:, 128:129]).then_inc(nsem[h], 1)
+        P.wait_ge(tsem[h], 1)
+        P.matmul(pt[h][:, X0 + FG:X1 + 1], T.xs[FG:128, HB * h:HB * (h + 1)], T.idn[FG:128, X0 + FG:X1 + 1],
+                 True, True).then_inc(tsem[h], 1)
+    for h in range(2):
+        V.wait_ge(tsem[h], 2)
+        V.tensor_reduce(own[:, o + h:o + h + 1], pt[h][:, 0:X1 + 1:X1], AxisListType.X, ADD).then_inc(nsem[h], 1)
     for h in range(2):
         A.wait_ge(nsem[h], 1)
-        A.activation(T.junk[:, HB * h:HB * (h + 1)], pt[h][:, 0:128], F.Square, bias=own[:, o + h:o + h + 1], scale=1.0,
+        A.activation(T.junk[:, HB * h:HB * (h + 1)], pt[h][:, X0:X1], F.Square, bias=own[:, o + h:o + h + 1], scale=1.0,
                      accum_out=own[:, o + 2 + h:o + 3 + h]).then_inc(S.st, 1)
 
     g.wait_ge(S.n0, 1)
     g.wait_ge(S.n1, 1)
     g.wait_ge(S.st, 2)
     slot = T.land[:, W * rank:W * (rank + 1)]
+    R = T.res
     if is_hub:
         sent = _send(g, T, topo, core, [h for h in hubs if h != core], slot, slot, NE)
         need = NE * (len(cores) - 1)
-        g.wait_ge(S.arr, need)
-        if serve[core]:
-            sent += _send(g, T, topo, core, serve[core], T.land[:, :], T.land[:, :], NE)
     else:
         sent = _send(g, T, topo, core, hubs, T.stat[:, :], slot, NE)
         need = NE
 
-    sm, L = T.sm, T.land
-    n_all = W * NR
-    A.wait_ge(S.st, 2)
-    A.activation(sm[:, 16:18], own[:, o + 2:o + 4], F.Sqrt, bias=EPS, scale=1.0 / (128.0 * NR)).then_inc(S.ia, 1)
-    V.wait_ge(S.ia, 1)
-    V.reciprocal(sm[:, 18:20], sm[:, 16:18]).then_inc(S.ib, 1)
-    V.wait_ge(S.ib, 1)
-    V.tensor_tensor(sm[:, 20:22], sm[:, 18:20], sm[:, 18:20], MUL).then_inc(S.ic, 1)
-    V.wait_ge(S.ic, 1)
-    V.tensor_scalar(sm[:, 22:24], sm[:, 20:22], 1.0 / float(NR * NR * NR), None, MUL).then_inc(S.ie, 1)
-    V.tensor_scalar(sm[:, 24:26], sm[:, 20:22], 1.0 / (128.0 * NR), None, MUL).then_inc(S.ie, 1)
-    V.tensor_scalar(sm[:, 26:28], sm[:, 20:22], EPS, None, MUL).then_inc(S.ie, 1)
-    V.wait_ge(S.ie, 3)
+    if is_hub:
+        sm, L = T.sm, T.land
+        n_all = W * NR
+        A.wait_ge(S.st, 2)
+        A.activation(sm[:, 16:18], own[:, o + 2:o + 4], F.Sqrt, bias=EPS, scale=1.0 / (128.0 * NR)).then_inc(S.ia, 1)
+        V.wait_ge(S.st, 2)
+        V.tensor_scalar(sm[:, 28:30], own[:, o + 2:o + 4], 1.0 / (128.0 * NR), EPS, MUL, ADD).then_inc(S.ib, 1)
+        V.wait_ge(S.ib, 1)
+        V.reciprocal(sm[:, 20:22], sm[:, 28:30]).then_inc(S.ic, 1)
+        V.wait_ge(S.ic, 1)
+        V.tensor_scalar(sm[:, 22:24], sm[:, 20:22], 1.0 / float(NR * NR * NR), None, MUL).then_inc(S.ie, 1)
+        V.tensor_scalar(sm[:, 24:26], sm[:, 20:22], 1.0 / (128.0 * NR), None, MUL).then_inc(S.ie, 1)
+        V.tensor_scalar(sm[:, 26:28], sm[:, 20:22], EPS, None, MUL).then_inc(S.ie, 1)
+        V.wait_ge(S.ie, 3)
 
-    V.wait_ge(S.arr, need)
-    V.wait_ge(S.n0, 1)
-    V.wait_ge(S.n1, 1)
-    V.wait_ge(S.st, 2)
-    for h in range(2):
-        V.tensor_reduce(sm[:, h:h + 1], L[:, h:n_all:W], AxisListType.X, ADD, negate=True).then_inc(rsem[h], 1)
-    for h in range(2):
-        V.tensor_reduce(sm[:, 2 + h:3 + h], L[:, 2 + h:n_all:W], AxisListType.X, ADD).then_inc(S.qs, 1)
-    V.wait_ge(S.qs, 2)
-    for h in range(2):
-        V.tensor_scalar(sm[:, 4 + h:5 + h], sm[:, 2 + h:3 + h], sm[:, 24 + h:25 + h], sm[:, 26 + h:27 + h],
-                        MUL, ADD).then_inc(S.qe, 1)
-    V.wait_ge(S.r0, 1)
-    V.wait_ge(S.r1, 1)
-    V.tensor_scalar(sm[:, 6:8], sm[:, 0:2], -1.0 / NR, None, MUL).then_inc(S.nm, 1)
+        V.wait_ge(S.arr, need)
+        V.wait_ge(S.n0, 1)
+        V.wait_ge(S.n1, 1)
+        for h in range(2):
+            V.tensor_reduce(sm[:, h:h + 1], L[:, h:n_all:W], AxisListType.X, ADD, negate=True).then_inc(rsem[h], 1)
+        for h in range(2):
+            V.tensor_reduce(sm[:, 2 + h:3 + h], L[:, 2 + h:n_all:W], AxisListType.X, ADD).then_inc(S.qs, 1)
+        V.wait_ge(S.qs, 2)
+        for h in range(2):
+            V.tensor_scalar(sm[:, 4 + h:5 + h], sm[:, 2 + h:3 + h], sm[:, 24 + h:25 + h], sm[:, 26 + h:27 + h],
+                            MUL, ADD).then_inc(S.qe, 1)
+        V.wait_ge(S.r0, 1)
+        V.wait_ge(S.r1, 1)
+        V.tensor_scalar(R[:, 0:2], sm[:, 0:2], -1.0 / NR, None, MUL).then_inc(S.nm, 1)
 
-    A.wait_ge(S.arr, need)
-    for h in range(2):
-        A.wait_ge(rsem[h], 1)
-        A.activation(T.junk[:, 2 * HB + 16 * h:2 * HB + 16 * h + NR], L[:, h:n_all:W], F.Square, bias=sm[:, h:h + 1],
-                     scale=float(NR), accum_out=sm[:, 8 + h:9 + h]).then_inc(S.bb, 1)
-    A.wait_ge(S.bb, 2)
-    A.wait_ge(S.qe, 2)
-    A.wait_ge(S.ie, 3)
-    for h in range(2):
-        A.activation(sm[:, 10 + h:11 + h], sm[:, 8 + h:9 + h], F.Sqrt, bias=sm[:, 4 + h:5 + h],
-                     scale=sm[:, 22 + h:23 + h]).then_inc(S.sq, 1)
+        A.wait_ge(S.arr, need)
+        for h in range(2):
+            A.wait_ge(rsem[h], 1)
+            A.activation(T.junk[:, 2 * HB + 16 * h:2 * HB + 16 * h + NR], L[:, h:n_all:W], F.Square,
+                         bias=sm[:, h:h + 1], scale=float(NR), accum_out=sm[:, 8 + h:9 + h]).then_inc(S.bb, 1)
+        A.wait_ge(S.bb, 2)
+        A.wait_ge(S.qe, 2)
+        A.wait_ge(S.ie, 3)
+        for h in range(2):
+            A.activation(sm[:, 10 + h:11 + h], sm[:, 8 + h:9 + h], F.Sqrt, bias=sm[:, 4 + h:5 + h],
+                         scale=sm[:, 22 + h:23 + h]).then_inc(S.sq, 1)
 
-    V.wait_ge(S.sq, 2)
-    V.reciprocal(sm[:, 12:14], sm[:, 10:12]).then_inc(S.rc, 1)
-    V.wait_ge(S.rc, 1)
-    V.tensor_tensor(sm[:, 14:16], sm[:, 12:14], sm[:, 18:20], MUL).then_inc(S.rs, 1)
-    V.wait_ge(S.rs, 1)
-    V.wait_ge(S.nm, 1)
+        V.wait_ge(S.sq, 2)
+        V.wait_ge(S.ia, 1)
+        V.tensor_tensor(sm[:, 12:14], sm[:, 10:12], sm[:, 16:18], MUL).then_inc(S.rc, 1)
+        V.wait_ge(S.rc, 1)
+        V.reciprocal(R[:, 2:4], sm[:, 12:14]).then_inc(S.rs, 1)
+        V.wait_ge(S.rs, 1)
+        V.wait_ge(S.nm, 1)
+        if serve[core]:
+            g.wait_ge(S.nm, 1)
+            g.wait_ge(S.rs, 1)
+            sent += _send(g, T, topo, core, serve[core], R[:, :], R[:, :], NE)
+    else:
+        V.wait_ge(S.arr, need)
+        V.wait_ge(S.st, 2)
+
     for h in range(2):
-        V.tensor_scalar(T.yt[:, HB * h:HB * (h + 1)], pt[h][:, 0:128], sm[:, 6 + h:7 + h], sm[:, 14 + h:15 + h],
+        V.tensor_scalar(T.yt[:, HB * h:HB * (h + 1)], pt[h][:, X0:X1], R[:, h:h + 1], R[:, 2 + h:3 + h],
                         ADD, MUL).then_inc(ysem[h], 1)
     for h in range(2):
         P.wait_ge(ysem[h], 1)
-        P.matmul(py[h][:, 0:128], T.yt[:, HB * h:HB * (h + 1)], T.idn[:, 0:128], True, True).then_inc(usem[h], 1)
+        P.matmul(py[h][:, 0:128], T.yt[:, HB * h:HB * (h + 1)], T.idn[:, X0:X1], True, True).then_inc(usem[h], 1)
     for h in range(2):
         V.wait_ge(usem[h], 1)
         V.tensor_copy(T.ys[:, HB * h:HB * (h + 1)], py[h][:, 0:128]).then_inc(csem[h], 1)

from concourse.bass import DstId, RemoteDMATransfer
from concourse.mybir import AluOpType, AxisListType, ActivationFunctionType

NR = 9
TK = 256
HB = 128
FG = 64
EPS = 0.01
W = 4

SCRATCH = {
    "xs":   ("sbuf", [128, TK], "float32"),
    "ones": ("sbuf", [128, 128], "float32"),
    "idn":  ("sbuf", [128, 132], "float32"),
    "stat": ("sbuf", [128, W], "float32"),
    "land": ("sbuf", [128, W * NR], "float32"),
    "res":  ("sbuf", [128, W], "float32"),
    "junk": ("sbuf", [128, 2 * HB + 32], "float32"),
    "sm":   ("sbuf", [128, 32], "float32"),
    "yt":   ("sbuf", [128, TK], "float32"),
    "ys":   ("sbuf", [128, TK], "float32"),
    "pt0":  ("psum", [128, 512], "float32"),
    "pt1":  ("psum", [128, 512], "float32"),
    "py0":  ("psum", [128, 512], "float32"),
    "py1":  ("psum", [128, 512], "float32"),
}
SEMAPHORES = ["la", "lb", "ca", "cb", "t0", "t1", "n0", "n1", "st", "arr", "sent", "r0", "r1", "qs", "qe", "nm", "bb",
              "sq", "rc", "rs", "ia", "ib", "ic", "ie", "y0", "y1", "u0", "u1", "c0", "c1", "so0", "so1"]


def _plan(cores, topo):
    hubs = [c for c in cores if all(topo.may_write(c, d) and topo.may_write(d, c) for d in cores if d != c)]
    leaves = [c for c in cores if c not in hubs]
    serve = {h: [] for h in hubs}
    near = [l for l in leaves if topo.rack(topo.host(l)) == topo.rack(topo.host(hubs[0]))]
    for l in near + [l for l in leaves if l not in near]:
        level = min(hubs.index(h) + len(serve[h]) for h in hubs)
        cand = [h for h in hubs if hubs.index(h) + len(serve[h]) == level]
        same = [h for h in cand if topo.chip(h) == topo.chip(l)]
        serve[(same or cand)[0]].append(l)
    return hubs, leaves, serve


def _engines(topo, src, dsts, n):
    m = topo.mask(src, dsts[0])
    for d in dsts[1:]:
        m &= topo.mask(src, d)
    out, k, b = 0, 0, 0
    while k < n and (m >> b):
        if (m >> b) & 1:
            out |= 1 << b
            k += 1
        b += 1
    return out, k


def _send(g, T, topo, core, dsts, src, dst, n_eng):
    mask, k = _engines(topo, core, dsts, n_eng)
    ids = []
    for d in dsts:
        rid, pid = topo.addr(d, core)
        ids.append(DstId(rid=rid, pnc=pid))
    g.remote_dma_fused([RemoteDMATransfer(dst_ids=ids, dma_engine_mask=mask, remote_sem=T.sem.arr,
                                          srcs=[src], dsts=[dst for _ in dsts], alu_op=0)], local_sem=T.sem.sent)
    return k


def rank_program(g, core, T, topo):
    rank = T.rank_of(core)
    if rank is None:
        return
    cores = list(T.cores)
    hubs, leaves, serve = _plan(cores, topo)
    is_hub = core in hubs
    S = T.sem
    V, A, P = g.vector, g.scalar, g.tensor
    ADD, MUL = AluOpType.add, AluOpType.mult
    F = ActivationFunctionType
    NE = 8
    pt = [T.pt0, T.pt1]
    py = [T.py0, T.py1]
    tsem, nsem, rsem = [S.t0, S.t1], [S.n0, S.n1], [S.r0, S.r1]
    ysem, usem, csem, osem = [S.y0, S.y1], [S.u0, S.u1], [S.c0, S.c1], [S.so0, S.so1]
    own, o = (T.land, W * rank) if is_hub else (T.stat, 0)
    X0, X1 = 1, 1 + 128

    g.sync.dma_start(T.xs[0:FG, :], T.x[0:FG, :]).then_inc(S.la, 16)
    g.scalar.dma_start(T.xs[FG:128, :], T.x[FG:128, :]).then_inc(S.lb, 16)
    V.memset(T.ones[:, :], 1.0).then_inc(S.ca, 1)
    V.memset(T.idn[:, 0:1], -1.0 / 128.0).then_inc(S.cb, 1)
    V.memset(T.idn[:, X1:X1 + 1], -1.0 / 128.0).then_inc(S.cb, 1)
    g.wait_ge(S.ca, 1)
    g.affine_select(T.idn[:, X0:X1], T.ones[:, :], [[-1, 128]], AluOpType.is_equal, 0.0, 0, 1).then_inc(S.cb, 1)

    P.wait_ge(S.cb, 3)
    P.wait_ge(S.la, 16)
    for h in range(2):
        P.matmul(pt[h][:, 0:X0 + FG], T.xs[0:FG, HB * h:HB * (h + 1)], T.idn[0:FG, 0:X0 + FG],
                 True, True).then_inc(tsem[h], 1)
    P.wait_ge(S.lb, 16)
    for h in range(2):
        P.wait_ge(tsem[h], 1)
        P.matmul(pt[h][:, X0 + FG:X1 + 1], T.xs[FG:128, HB * h:HB * (h + 1)], T.idn[FG:128, X0 + FG:X1 + 1],
                 True, True).then_inc(tsem[h], 1)
    for h in range(2):
        V.wait_ge(tsem[h], 2)
        V.tensor_reduce(own[:, o + h:o + h + 1], pt[h][:, 0:X1 + 1:X1], AxisListType.X, ADD).then_inc(nsem[h], 1)
    for h in range(2):
        A.wait_ge(nsem[h], 1)
        A.activation(T.junk[:, HB * h:HB * (h + 1)], pt[h][:, X0:X1], F.Square, bias=own[:, o + h:o + h + 1], scale=1.0,
                     accum_out=own[:, o + 2 + h:o + 3 + h]).then_inc(S.st, 1)

    g.wait_ge(S.n0, 1)
    g.wait_ge(S.n1, 1)
    g.wait_ge(S.st, 2)
    slot = T.land[:, W * rank:W * (rank + 1)]
    R = T.res
    if is_hub:
        sent = _send(g, T, topo, core, [h for h in hubs if h != core], slot, slot, NE)
        need = NE * (len(cores) - 1)
    else:
        sent = _send(g, T, topo, core, hubs, T.stat[:, :], slot, NE)
        need = NE

    if is_hub:
        sm, L = T.sm, T.land
        n_all = W * NR
        A.wait_ge(S.st, 2)
        A.activation(sm[:, 16:18], own[:, o + 2:o + 4], F.Sqrt, bias=EPS, scale=1.0 / (128.0 * NR)).then_inc(S.ia, 1)
        V.wait_ge(S.st, 2)
        V.tensor_scalar(sm[:, 28:30], own[:, o + 2:o + 4], 1.0 / (128.0 * NR), EPS, MUL, ADD).then_inc(S.ib, 1)
        V.wait_ge(S.ib, 1)
        V.reciprocal(sm[:, 20:22], sm[:, 28:30]).then_inc(S.ic, 1)
        V.wait_ge(S.ic, 1)
        V.tensor_scalar(sm[:, 22:24], sm[:, 20:22], 1.0 / float(NR * NR * NR), None, MUL).then_inc(S.ie, 1)
        V.tensor_scalar(sm[:, 24:26], sm[:, 20:22], 1.0 / (128.0 * NR), None, MUL).then_inc(S.ie, 1)
        V.tensor_scalar(sm[:, 26:28], sm[:, 20:22], EPS, None, MUL).then_inc(S.ie, 1)
        V.wait_ge(S.ie, 3)

        V.wait_ge(S.arr, need)
        V.wait_ge(S.n0, 1)
        V.wait_ge(S.n1, 1)
        for h in range(2):
            V.tensor_reduce(sm[:, h:h + 1], L[:, h:n_all:W], AxisListType.X, ADD, negate=True).then_inc(rsem[h], 1)
        for h in range(2):
            V.tensor_reduce(sm[:, 2 + h:3 + h], L[:, 2 + h:n_all:W], AxisListType.X, ADD).then_inc(S.qs, 1)
        V.wait_ge(S.qs, 2)
        for h in range(2):
            V.tensor_scalar(sm[:, 4 + h:5 + h], sm[:, 2 + h:3 + h], sm[:, 24 + h:25 + h], sm[:, 26 + h:27 + h],
                            MUL, ADD).then_inc(S.qe, 1)
        V.wait_ge(S.r0, 1)
        V.wait_ge(S.r1, 1)
        V.tensor_scalar(R[:, 0:2], sm[:, 0:2], -1.0 / NR, None, MUL).then_inc(S.nm, 1)

        A.wait_ge(S.arr, need)
        for h in range(2):
            A.wait_ge(rsem[h], 1)
            A.activation(T.junk[:, 2 * HB + 16 * h:2 * HB + 16 * h + NR], L[:, h:n_all:W], F.Square,
                         bias=sm[:, h:h + 1], scale=float(NR), accum_out=sm[:, 8 + h:9 + h]).then_inc(S.bb, 1)
        A.wait_ge(S.bb, 2)
        A.wait_ge(S.qe, 2)
        A.wait_ge(S.ie, 3)
        for h in range(2):
            A.activation(sm[:, 10 + h:11 + h], sm[:, 8 + h:9 + h], F.Sqrt, bias=sm[:, 4 + h:5 + h],
                         scale=sm[:, 22 + h:23 + h]).then_inc(S.sq, 1)

        V.wait_ge(S.sq, 2)
        V.wait_ge(S.ia, 1)
        V.tensor_tensor(sm[:, 12:14], sm[:, 10:12], sm[:, 16:18], MUL).then_inc(S.rc, 1)
        V.wait_ge(S.rc, 1)
        V.reciprocal(R[:, 2:4], sm[:, 12:14]).then_inc(S.rs, 1)
        V.wait_ge(S.rs, 1)
        V.wait_ge(S.nm, 1)
        if serve[core]:
            g.wait_ge(S.nm, 1)
            g.wait_ge(S.rs, 1)
            sent += _send(g, T, topo, core, serve[core], R[:, :], R[:, :], NE)
    else:
        V.wait_ge(S.arr, need)
        V.wait_ge(S.st, 2)

    for h in range(2):
        V.tensor_scalar(T.yt[:, HB * h:HB * (h + 1)], pt[h][:, X0:X1], R[:, h:h + 1], R[:, 2 + h:3 + h],
                        ADD, MUL).then_inc(ysem[h], 1)
    for h in range(2):
        P.wait_ge(ysem[h], 1)
        P.matmul(py[h][:, 0:128], T.yt[:, HB * h:HB * (h + 1)], T.idn[:, X0:X1], True, True).then_inc(usem[h], 1)
    for h in range(2):
        V.wait_ge(usem[h], 1)
        V.tensor_copy(T.ys[:, HB * h:HB * (h + 1)], py[h][:, 0:128]).then_inc(csem[h], 1)
    for h, q in ((0, g.sync), (1, g.scalar)):
        q.wait_ge(csem[h], 1)
        q.dma_start(T.y[:, HB * h:HB * (h + 1)], T.ys[:, HB * h:HB * (h + 1)]).then_inc(osem[h], 16)
        q.wait_ge(osem[h], 16)
    g.wait_ge(S.sent, sent)
